import numpy as np
import ml_dtypes


def mxq(x, axis, fmt="e4m3"):
    dtype, down = {"e4m3": (ml_dtypes.float8_e4m3fn, 7), "e5m2": (ml_dtypes.float8_e5m2, 14)}[fmt]
    v = np.moveaxis(np.asarray(x, np.float32).astype(ml_dtypes.bfloat16).astype(np.float64), axis, -1)
    blocks = v.reshape(v.shape[:-1] + (-1, 32))
    amax = np.abs(blocks).max(-1, keepdims=True)
    byte = np.maximum(np.where(amax > 0, np.frexp(amax)[1] - 1 + 127, 0) - down, 1)
    scale = np.exp2(byte - 127.0)
    codes = (blocks / scale).astype(np.float32).astype(dtype).astype(np.float64)
    return np.moveaxis((codes * scale).reshape(v.shape), -1, axis)


WIDE = False


def mx_kscale(k, group=512):
    if not WIDE:
        return np.ones(k)
    levels = np.array([10, -10, 5, -5, 0])
    if group != 512:
        return np.exp2(np.random.permutation(np.resize(levels, k // group))).repeat(group)
    if k % 512:
        return np.exp2(np.random.permutation(np.resize(levels, k // 32))).repeat(32)
    a = np.empty((k // 512, 16))
    for p in range(k // 512):
        a[p, :8] = np.random.permutation(np.resize(levels, 8))
        for g in range(8):
            far = levels[np.abs(levels - a[p, g]) >= 10]
            a[p, g + 8] = far[np.random.randint(len(far))]
    return np.exp2(a.ravel()).repeat(32)


def f64(x):
    return np.asarray(x).astype(np.float64)


def striped(idx):
    return np.tile(np.asarray(idx).reshape(-1, 16).T, (8, 1)).astype(np.uint16)


def unstriped(offs):
    return offs[:16].T.reshape(-1).astype(np.int64)


H, KV, D, NQ, N = 4, 2, 256, 512, 512
CAP = 2.0


def setup_inputs():
    n = np.random.standard_normal
    s = mx_kscale(D, 0)[:, None]
    u = mx_kscale(N)
    t = np.random.uniform(0.5, 2.0, N) * u
    v = n((KV, N, 128))
    v[:, :, 127] = 1.0
    return {
        "qT": (n((H, D, NQ)) * s * (0.70 / np.sqrt(D))).astype(np.float32),
        "kT": (n((KV, D, N)) / s).astype(np.float32),
        "t": t.reshape(N, 1).astype(np.float32),
        "v": (v / t[:, None]).astype(np.float32),
        "kb": (0.5 * n((N, 1))).astype(np.float32),
        "og": n((H, NQ, 128)).astype(np.float32),
    }


def reference(qT, kT, t, v, kb, og):
    a = np.repeat(mxq(f64(kT), 1, "e4m3"), H // KV, 0).transpose(0, 2, 1) @ mxq(f64(qT), 1, "e4m3")
    a = a + f64(kb)
    a = CAP * np.tanh(a / CAP)
    p = np.exp(a)
    w = p * f64(t)
    y = mxq(w, 1, "e4m3").transpose(0, 2, 1) @ np.repeat(mxq(f64(v), 1, "e4m3"), H // KV, 0)
    y = y / (y[:, :, 127:128])
    y = y / (1.0 + np.exp(-f64(og)))
    return y

@@ -1,0 +1,314 @@
+from contextlib import ExitStack
+
+import concourse.mybir as mybir
+
+H, KV, D, NQ, N, E = 4, 2, 256, 512, 512, 128
+CAP = 2.0
+FLOPS = 2 * H * NQ * N * (D + E)
+
+F32 = mybir.dt.float32
+BF16 = mybir.dt.bfloat16
+U32 = mybir.dt.uint32
+I32 = mybir.dt.int32
+U8 = mybir.dt.uint8
+FP8X4 = mybir.dt.float8_e4m3fn_x4
+ACT = mybir.ActivationFunctionType
+ALU = mybir.AluOpType
+
+P = 128
+HALF = 64
+PACK = 4
+NB = 128
+SCORE_BANKS = 3
+LN_HI = 2.0 ** 64
+LN_LO = 2.0 ** -64
+TINY = 2.0 ** -126
+Q_FIRST = 256
+Q_FIRST_VECTOR = 160
+
+UNITS = [
+    (0, 0, 256, [256]),
+    (0, 256, 256, [256]),
+    (1, 0, 512, [512]),
+    (2, 0, 512, [256, 256]),
+    (3, 0, 256, [256]),
+    (3, 256, 256, [128, 128]),
+]
+
+
+def tile_rows_a_exp_kb_cap_gate_kernel(tc, qT, kT, t, v, kb, og, out):
+    nc = tc.nc
+    with ExitStack() as ctx:
+        sb = ctx.enter_context(tc.tile_pool(name="sb", bufs=1))
+        ps = ctx.enter_context(tc.psum_pool(name="ps", bufs=1))
+        ctx.enter_context(tc.manual_schedule())
+
+        def quantize(codes, scales, grouped):
+            nc.vector.quantize_mx(out=codes.bitcast(FP8X4), scales=scales, in_=grouped)
+
+        def interleave(engine_copy, grouped, rows):
+            engine_copy(
+                out=grouped.rearrange("p (c i) j -> p c j i", i=PACK),
+                in_=rows.rearrange("p j (c i) -> p c j i", i=PACK),
+            )
+
+        k_pack = sb.tile([P, N + N // 4], U32, name="k_pack", align_bytes=64)
+        k_swap = sb.tile([P, N + N // 4], U32, name="k_swap", align_bytes=64)
+        nc.gpsimd.memset(k_pack[:, N:], 0)
+
+        q_rows = qT.rearrange("(g h) (p j) n -> g (h p) j n", h=2, j=PACK)
+        og_sb = {}
+
+        def load_gate(queue, u):
+            h, q0, nq, chunks = UNITS[u]
+            og_sb[u] = sb.tile([P, nq // NB, E], F32, name="og%d" % u)
+            queue.dma_start(out=og_sb[u][:], in_=og[h, q0 : q0 + nq, :].rearrange("(c p) e -> p c e", p=P))
+
+        t_sb = sb.tile([P, PACK], F32, name="t_sb")
+        kb_sb = sb.tile([P, PACK], F32, name="kb_sb")
+        nc.scalar.dma_start(out=t_sb[:], in_=t.rearrange("(p j) o -> p (j o)", j=PACK))
+        nc.scalar.dma_start(out=kb_sb[:], in_=kb.rearrange("(p j) o -> p (j o)", j=PACK))
+        load_gate(nc.scalar, 0)
+
+        k_raw = sb.tile([P, PACK, N], F32, name="k_raw")
+        nc.sync.dma_start(out=k_raw[:], in_=kT.rearrange("g (p j) n -> (g p) j n", j=PACK))
+        qa_raw = sb.tile([P, PACK, Q_FIRST], F32, name="qa_raw")
+        nc.sync.dma_start(out=qa_raw[:], in_=q_rows[0][:, :, :Q_FIRST])
+        load_gate(nc.sync, 1)
+        qb_raw = sb.tile([P, PACK, NQ - Q_FIRST], F32, name="qb_raw")
+        nc.sync.dma_start(out=qb_raw[:], in_=q_rows[0][:, :, Q_FIRST:])
+        v_raw = sb.tile([P, KV, PACK * E], F32, name="v_raw")
+        nc.sync.dma_start(out=v_raw[:], in_=v.rearrange("g (p j) e -> p g (j e)", j=PACK))
+
+        t_abs = sb.tile([P, PACK], F32, name="t_abs")
+        nc.vector.scalar_tensor_tensor(out=t_abs[:], in0=t_sb[:], scalar=-1.0, in1=t_sb[:], op0=ALU.mult, op1=ALU.max)
+        t_pos = sb.tile([P, PACK], F32, name="t_pos")
+        nc.vector.tensor_scalar(out=t_pos[:], in0=t_sb[:], scalar1=0.0, scalar2=2.0, op0=ALU.is_ge, op1=ALU.mult)
+        t_rng = sb.tile([P, 3, PACK], F32, name="t_rng")
+        nc.vector.tensor_scalar(out=t_rng[:, 0, :], in0=t_abs[:], scalar1=LN_LO, scalar2=LN_HI, op0=ALU.max, op1=ALU.min)
+        nc.vector.tensor_scalar(out=t_rng[:, 1, :], in0=t_abs[:], scalar1=LN_HI, scalar2=LN_LO, op0=ALU.max, op1=ALU.mult)
+        nc.vector.tensor_scalar(out=t_rng[:, 2, :], in0=t_abs[:], scalar1=TINY, scalar2=LN_LO, op0=ALU.max, op1=ALU.min)
+        t_sign = sb.tile([P, PACK], F32, name="t_sign")
+        nc.vector.tensor_scalar(out=t_sign[:], in0=t_pos[:], scalar1=-1.0, scalar2=None, op0=ALU.add)
+        kb_cap = sb.tile([P, PACK], F32, name="kb_cap")
+        nc.vector.tensor_scalar(out=kb_cap[:], in0=kb_sb[:], scalar1=1.0 / CAP, scalar2=None, op0=ALU.mult)
+        ln_rng = sb.tile([P, 3, PACK], F32, name="ln_rng")
+        nc.scalar.activation(out=ln_rng[:, 0:2, :], in_=t_rng[:, 0:2, :], func=ACT.Ln)
+        nc.scalar.activation(out=ln_rng[:, 2, :], in_=t_rng[:, 2, :], func=ACT.Ln, scale=LN_HI)
+        ln_t = sb.tile([P, PACK], F32, name="ln_t")
+
+        half_tanh = {}
+        gate = {}
+
+        def gate_tanh(u):
+            half_tanh[u] = sb.tile([P, UNITS[u][2] // NB, E], F32, name="gt%d" % u)
+            nc.scalar.activation(out=half_tanh[u][:], in_=og_sb[u][:], func=ACT.Tanh, scale=0.5)
+
+        def gate_affine(u):
+            gate[u] = sb.tile([P, UNITS[u][2] // NB, E], F32, name="gate%d" % u)
+            nc.vector.tensor_scalar(out=gate[u][:], in0=half_tanh[u][:], scalar1=0.5, scalar2=0.5, op0=ALU.mult, op1=ALU.add)
+
+        gate_tanh(0)
+
+        k_bf = sb.tile([P, PACK, NB, PACK], BF16, name="k_bf", align_bytes=64)
+        nc.vector.tensor_copy(
+            out=k_bf[:].rearrange("p r s j -> p s j r"),
+            in_=k_raw[:].rearrange("p j (s r) -> p s j r", r=PACK),
+        )
+        nc.vector.tensor_reduce(out=ln_t[:], in_=ln_rng[:].rearrange("p a j -> p j a"), axis=mybir.AxisListType.X, op=ALU.add)
+
+        def k_codes(pack, r0, r1):
+            return pack[:, r0 * NB : r1 * NB]
+
+        def k_scales(pack, r0, r1):
+            return pack[:, N + r0 * NB // 4 : N + r1 * NB // 4].bitcast(U8)
+
+        def quantize_keys(r0, r1):
+            quantize(k_codes(k_pack, r0, r1), k_scales(k_pack, r0, r1), k_bf[:, r0:r1].rearrange("p r s j -> p (r s j)"))
+
+        q_blocks = {}
+
+        def query_tiles(name, n):
+            grouped = sb.tile([P, n, PACK], BF16, name=name + "_bf", align_bytes=64)
+            codes = sb.tile([P, n], U32, name=name + "_codes", align_bytes=64)
+            scales = sb.tile([P, n], U8, name=name + "_scales", align_bytes=64)
+            return grouped, codes, scales
+
+        def quantize_queries(tiles, pair, q0, n):
+            grouped, codes, scales = tiles
+            quantize(codes[:], scales[:], grouped[:].rearrange("p n j -> p (n j)"))
+            for b in range(n // NB):
+                q_blocks[pair, q0 // NB + b] = (codes[:, b * NB : (b + 1) * NB], scales[:, b * NB : (b + 1) * NB])
+
+        qa = query_tiles("qa", Q_FIRST)
+        interleave(nc.vector.tensor_copy, qa[0][:, :Q_FIRST_VECTOR], qa_raw[:, :, :Q_FIRST_VECTOR])
+        interleave(nc.scalar.copy, qa[0][:, Q_FIRST_VECTOR:], qa_raw[:, :, Q_FIRST_VECTOR:])
+        gate_tanh(1)
+        quantize_keys(0, 1)
+        quantize_queries(qa, 0, 0, Q_FIRST)
+        quantize_keys(1, 2)
+        quantize_keys(2, 4)
+
+        nc.sync.dma_start(out=k_swap[HALF:, :].bitcast(I32), in_=k_pack[:HALF, :].bitcast(I32))
+        nc.sync.dma_start(out=k_swap[:HALF, :].bitcast(I32), in_=k_pack[HALF:, :].bitcast(I32))
+        qc_raw = sb.tile([P, PACK, NQ], F32, name="qc_raw")
+        nc.sync.dma_start(out=qc_raw[:], in_=q_rows[1])
+        for u in range(2, len(UNITS)):
+            load_gate(nc.sync, u)
+
+        qb = query_tiles("qb", NQ - Q_FIRST)
+        qc = query_tiles("qc", NQ)
+        v_bf = sb.tile([P, KV, E, PACK], BF16, name="v_bf", align_bytes=64)
+        v_codes = sb.tile([P, KV * E], U32, name="v_codes", align_bytes=64)
+        v_scales = sb.tile([P, KV * E], U8, name="v_scales", align_bytes=64)
+
+        steps = [(u, r) for u in range(len(UNITS)) for r in range(PACK)]
+        banks = {}
+        free_banks = [SCORE_BANKS, SCORE_BANKS]
+        pending = list(steps)
+
+        def issue_scores():
+            while pending:
+                u, r = pending[0]
+                h, q0, nq, chunks = UNITS[u]
+                side = h % 2
+                blocks = [(h // 2, b) for b in range(q0 // NB, (q0 + nq) // NB)]
+                if free_banks[side] == 0 or any(b not in q_blocks for b in blocks):
+                    return
+                pending.remove((u, r))
+                free_banks[side] = free_banks[side] - 1
+                rows = slice(side * HALF, (side + 1) * HALF)
+                pack = k_pack if side == h // 2 else k_swap
+                bank = ps.tile([P, 4 * NB], F32, name="scores%d" % side, tag="scores%d" % side, bufs=SCORE_BANKS)
+                banks[u, r] = bank
+                for i, b in enumerate(blocks):
+                    codes, scales = q_blocks[b]
+                    nc.tensor.matmul_mx(
+                        out=bank[:, i * NB : (i + 1) * NB],
+                        lhsT=k_codes(pack, r, r + 1)[rows, :].bitcast(FP8X4),
+                        lhsT_scale=k_scales(pack, r, r + 1)[rows, :],
+                        rhs=codes[rows, :].bitcast(FP8X4),
+                        rhs_scale=scales[rows, :],
+                        start=True,
+                        stop=True,
+                    )
+
+        capped = {}
+
+        def cap_scores(u):
+            h, q0, nq, chunks = UNITS[u]
+            capped[u] = sb.tile([P, PACK, nq], F32, name="cap%d" % u)
+            for r in range(PACK):
+                issue_scores()
+                nc.scalar.activation(
+                    out=capped[u][:, r, :], in_=banks[u, r][:, :nq], func=ACT.Tanh, bias=kb_cap[:, r : r + 1], scale=1.0 / CAP
+                )
+                free_banks[h % 2] = free_banks[h % 2] + 1
+            issue_scores()
+
+        weights = {}
+
+        def exp_chunk(c):
+            u, c0, n = c
+            weights[c] = sb.tile([P, PACK, n], BF16, name="w%d_%d" % (u, c0))
+            for r in range(PACK):
+                nc.scalar.activation(
+                    out=weights[c][:, r, :], in_=capped[u][:, r, c0 : c0 + n], func=ACT.Exp, bias=ln_t[:, r : r + 1], scale=CAP
+                )
+
+        w_tiles = {}
+        y_banks = {}
+        inv_den = {}
+
+        def group_weights(c):
+            u, c0, n = c
+            w_tiles[c] = query_tiles("wq%d_%d" % (u, c0), n)
+            interleave(nc.vector.tensor_copy, w_tiles[c][0][:], weights[c][:])
+
+        def second_product(c):
+            u, c0, n = c
+            g = UNITS[u][0] // 2
+            grouped, codes, scales = w_tiles[c]
+            quantize(codes[:], scales[:], grouped[:].rearrange("p n j -> p (n j)"))
+            y = ps.tile([P, 4, E], F32, name="y", tag="y", bufs=2)
+            y_banks[c] = y
+            for b in range(n // NB):
+                nc.tensor.matmul_mx(
+                    out=y[:, b, :],
+                    lhsT=codes[:, b * NB : (b + 1) * NB].bitcast(FP8X4),
+                    lhsT_scale=scales[:, b * NB : (b + 1) * NB],
+                    rhs=v_codes[:, g * E : (g + 1) * E].bitcast(FP8X4),
+                    rhs_scale=v_scales[:, g * E : (g + 1) * E],
+                    start=True,
+                    stop=True,
+                )
+
+        def invert_denominators(c):
+            u, c0, n = c
+            if u not in gate:
+                gate_affine(u)
+            inv_den[c] = sb.tile([P, n // NB], F32, name="inv%d_%d" % (u, c0))
+            nc.vector.reciprocal(out=inv_den[c][:], in_=y_banks[c][:, : n // NB, E - 1])
+
+        def finish(c):
+            u, c0, n = c
+            h, q0, nq, chunks = UNITS[u]
+            res = sb.tile([P, n // NB, E], F32, name="res%d_%d" % (u, c0))
+            for b in range(n // NB):
+                nc.vector.scalar_tensor_tensor(
+                    out=res[:, b, :],
+                    in0=y_banks[c][:, b, :],
+                    scalar=inv_den[c][:, b : b + 1],
+                    in1=gate[u][:, c0 // NB + b, :],
+                    op0=ALU.mult,
+                    op1=ALU.mult,
+                )
+            nc.sync.dma_start(out=out[h, q0 + c0 : q0 + c0 + n, :].rearrange("(c p) e -> p c e", p=P), in_=res[:])
+
+        last_chunk = []
+
+        def vector_slot(c):
+            group_weights(c)
+            for prev in last_chunk:
+                invert_denominators(prev)
+            second_product(c)
+            for prev in last_chunk:
+                finish(prev)
+            last_chunk.clear()
+            last_chunk.append(c)
+
+        def unit_chunks(u):
+            widths = UNITS[u][3]
+            return [(u, sum(widths[:i]), widths[i]) for i in range(len(widths))]
+
+        for u in range(len(UNITS)):
+            cap_scores(u)
+            if u == 0:
+                interleave(nc.vector.tensor_copy, qb[0][:], qb_raw[:])
+                gate_affine(0)
+                quantize_queries(qb, 0, Q_FIRST, NQ - Q_FIRST)
+                nc.vector.tensor_tensor(
+                    out=v_bf[:],
+                    in0=v_raw[:].rearrange("p g (j e) -> p g e j", j=PACK),
+                    in1=t_sign[:].unsqueeze(1).unsqueeze(1).to_broadcast([P, KV, E, PACK]),
+                    op=ALU.mult,
+                )
+                gate_affine(1)
+                quantize(v_codes[:], v_scales[:], v_bf[:].rearrange("p g e j -> p (g e j)"))
+                issue_scores()
+            if u == 2:
+                interleave(nc.vector.tensor_copy, qc[0][:], qc_raw[:])
+                quantize_queries(qc, 1, 0, NQ)
+                issue_scores()
+            if u > 0:
+                for c in unit_chunks(u - 1):
+                    vector_slot(c)
+            for c in unit_chunks(u):
+                exp_chunk(c)
+            if u >= 2:
+                gate_tanh(u)
+        for c in unit_chunks(len(UNITS) - 1):
+            vector_slot(c)
+        for prev in last_chunk:
+            invert_denominators(prev)
+            finish(prev)

@@ -24,7 +24,6 @@ LN_HI = 2.0 ** 64
 LN_LO = 2.0 ** -64
 TINY = 2.0 ** -126
 Q_FIRST = 256
-Q_FIRST_VECTOR = 160
 
 UNITS = [
     (0, 0, 256, [256]),
@@ -66,7 +65,7 @@ def tile_rows_a_exp_kb_cap_gate_kernel(tc, qT, kT, t, v, kb, og, out):
 
         t_sb = sb.tile([P, PACK], F32, name="t_sb")
         kb_sb = sb.tile([P, PACK], F32, name="kb_sb")
-        nc.scalar.dma_start(out=t_sb[:], in_=t.rearrange("(p j) o -> p (j o)", j=PACK))
+        nc.sync.dma_start(out=t_sb[:], in_=t.rearrange("(p j) o -> p (j o)", j=PACK))
         nc.scalar.dma_start(out=kb_sb[:], in_=kb.rearrange("(p j) o -> p (j o)", j=PACK))
         load_gate(nc.scalar, 0)
 
@@ -75,10 +74,9 @@ def tile_rows_a_exp_kb_cap_gate_kernel(tc, qT, kT, t, v, kb, og, out):
         qa_raw = sb.tile([P, PACK, Q_FIRST], F32, name="qa_raw")
         nc.sync.dma_start(out=qa_raw[:], in_=q_rows[0][:, :, :Q_FIRST])
         load_gate(nc.sync, 1)
+        load_gate(nc.sync, 2)
         qb_raw = sb.tile([P, PACK, NQ - Q_FIRST], F32, name="qb_raw")
         nc.sync.dma_start(out=qb_raw[:], in_=q_rows[0][:, :, Q_FIRST:])
-        v_raw = sb.tile([P, KV, PACK * E], F32, name="v_raw")
-        nc.sync.dma_start(out=v_raw[:], in_=v.rearrange("g (p j) e -> p g (j e)", j=PACK))
 
         t_abs = sb.tile([P, PACK], F32, name="t_abs")
         nc.vector.scalar_tensor_tensor(out=t_abs[:], in0=t_sb[:], scalar=-1.0, in1=t_sb[:], op0=ALU.mult, op1=ALU.max)
@@ -141,19 +139,21 @@ def tile_rows_a_exp_kb_cap_gate_kernel(tc, qT, kT, t, v, kb, og, out):
                 q_blocks[pair, q0 // NB + b] = (codes[:, b * NB : (b + 1) * NB], scales[:, b * NB : (b + 1) * NB])
 
         qa = query_tiles("qa", Q_FIRST)
-        interleave(nc.vector.tensor_copy, qa[0][:, :Q_FIRST_VECTOR], qa_raw[:, :, :Q_FIRST_VECTOR])
-        interleave(nc.scalar.copy, qa[0][:, Q_FIRST_VECTOR:], qa_raw[:, :, Q_FIRST_VECTOR:])
+        interleave(nc.vector.tensor_copy, qa[0][:], qa_raw[:])
         gate_tanh(1)
+        gate_tanh(2)
         quantize_keys(0, 1)
         quantize_queries(qa, 0, 0, Q_FIRST)
         quantize_keys(1, 2)
         quantize_keys(2, 4)
 
+        v_raw = sb.tile([P, KV, PACK * E], F32, name="v_raw")
+        nc.sync.dma_start(out=v_raw[:], in_=v.rearrange("g (p j) e -> p g (j e)", j=PACK))
         nc.sync.dma_start(out=k_swap[HALF:, :].bitcast(I32), in_=k_pack[:HALF, :].bitcast(I32))
-        nc.sync.dma_start(out=k_swap[:HALF, :].bitcast(I32), in_=k_pack[HALF:, :].bitcast(I32))
         qc_raw = sb.tile([P, PACK, NQ], F32, name="qc_raw")
         nc.sync.dma_start(out=qc_raw[:], in_=q_rows[1])
-        for u in range(2, len(UNITS)):
+        nc.sync.dma_start(out=k_swap[:HALF, :].bitcast(I32), in_=k_pack[HALF:, :].bitcast(I32))
+        for u in range(3, len(UNITS)):
             load_gate(nc.sync, u)
 
         qb = query_tiles("qb", NQ - Q_FIRST)
@@ -162,49 +162,56 @@ def tile_rows_a_exp_kb_cap_gate_kernel(tc, qT, kT, t, v, kb, og, out):
         v_codes = sb.tile([P, KV * E], U32, name="v_codes", align_bytes=64)
         v_scales = sb.tile([P, KV * E], U8, name="v_scales", align_bytes=64)
 
-        steps = [(u, r) for u in range(len(UNITS)) for r in range(PACK)]
+        def bank_groups(u):
+            if u == 0:
+                return [(0,), (1,), (2, 3)]
+            per_bank = 4 * NB // UNITS[u][2]
+            return [tuple(range(r, r + per_bank)) for r in range(0, PACK, per_bank)]
+
         banks = {}
         free_banks = [SCORE_BANKS, SCORE_BANKS]
-        pending = list(steps)
+        pending = [(u, places) for u in range(len(UNITS)) for places in bank_groups(u)]
 
-        def issue_scores():
-            while pending:
-                u, r = pending[0]
+        def issue_scores(last_unit):
+            while pending and pending[0][0] <= last_unit:
+                u, places = pending[0]
                 h, q0, nq, chunks = UNITS[u]
                 side = h % 2
                 blocks = [(h // 2, b) for b in range(q0 // NB, (q0 + nq) // NB)]
                 if free_banks[side] == 0 or any(b not in q_blocks for b in blocks):
                     return
-                pending.remove((u, r))
+                pending.remove((u, places))
                 free_banks[side] = free_banks[side] - 1
                 rows = slice(side * HALF, (side + 1) * HALF)
                 pack = k_pack if side == h // 2 else k_swap
                 bank = ps.tile([P, 4 * NB], F32, name="scores%d" % side, tag="scores%d" % side, bufs=SCORE_BANKS)
-                banks[u, r] = bank
-                for i, b in enumerate(blocks):
-                    codes, scales = q_blocks[b]
-                    nc.tensor.matmul_mx(
-                        out=bank[:, i * NB : (i + 1) * NB],
-                        lhsT=k_codes(pack, r, r + 1)[rows, :].bitcast(FP8X4),
-                        lhsT_scale=k_scales(pack, r, r + 1)[rows, :],
-                        rhs=codes[rows, :].bitcast(FP8X4),
-                        rhs_scale=scales[rows, :],
-                        start=True,
-                        stop=True,
-                    )
+                for slot, r in enumerate(places):
+                    banks[u, r] = bank[:, slot * nq : (slot + 1) * nq]
+                    for i, b in enumerate(blocks):
+                        codes, scales = q_blocks[b]
+                        nc.tensor.matmul_mx(
+                            out=banks[u, r][:, i * NB : (i + 1) * NB],
+                            lhsT=k_codes(pack, r, r + 1)[rows, :].bitcast(FP8X4),
+                            lhsT_scale=k_scales(pack, r, r + 1)[rows, :],
+                            rhs=codes[rows, :].bitcast(FP8X4),
+                            rhs_scale=scales[rows, :],
+                            start=True,
+                            stop=True,
+                        )
 
         capped = {}
 
         def cap_scores(u):
             h, q0, nq, chunks = UNITS[u]
             capped[u] = sb.tile([P, PACK, nq], F32, name="cap%d" % u)
-            for r in range(PACK):
-                issue_scores()
-                nc.scalar.activation(
-                    out=capped[u][:, r, :], in_=banks[u, r][:, :nq], func=ACT.Tanh, bias=kb_cap[:, r : r + 1], scale=1.0 / CAP
-                )
+            for places in bank_groups(u):
+                issue_scores(u + 1)
+                for r in places:
+                    nc.scalar.activation(
+                        out=capped[u][:, r, :], in_=banks[u, r], func=ACT.Tanh, bias=kb_cap[:, r : r + 1], scale=1.0 / CAP
+                    )
                 free_banks[h % 2] = free_banks[h % 2] + 1
-            issue_scores()
+            issue_scores(u + 1)
 
         weights = {}
 
@@ -225,11 +232,14 @@ def tile_rows_a_exp_kb_cap_gate_kernel(tc, qT, kT, t, v, kb, og, out):
             w_tiles[c] = query_tiles("wq%d_%d" % (u, c0), n)
             interleave(nc.vector.tensor_copy, w_tiles[c][0][:], weights[c][:])
 
+        def quantize_weights(c):
+            grouped, codes, scales = w_tiles[c]
+            quantize(codes[:], scales[:], grouped[:].rearrange("p n j -> p (n j)"))
+
         def second_product(c):
             u, c0, n = c
             g = UNITS[u][0] // 2
             grouped, codes, scales = w_tiles[c]
-            quantize(codes[:], scales[:], grouped[:].rearrange("p n j -> p (n j)"))
             y = ps.tile([P, 4, E], F32, name="y", tag="y", bufs=2)
             y_banks[c] = y
             for b in range(n // NB):
@@ -245,8 +255,6 @@ def tile_rows_a_exp_kb_cap_gate_kernel(tc, qT, kT, t, v, kb, og, out):
 
         def invert_denominators(c):
             u, c0, n = c
-            if u not in gate:
-                gate_affine(u)
             inv_den[c] = sb.tile([P, n // NB], F32, name="inv%d_%d" % (u, c0))
             nc.vector.reciprocal(out=inv_den[c][:], in_=y_banks[c][:, : n // NB, E - 1])
 
@@ -265,50 +273,93 @@ def tile_rows_a_exp_kb_cap_gate_kernel(tc, qT, kT, t, v, kb, og, out):
                 )
             nc.sync.dma_start(out=out[h, q0 + c0 : q0 + c0 + n, :].rearrange("(c p) e -> p c e", p=P), in_=res[:])
 
-        last_chunk = []
-
-        def vector_slot(c):
-            group_weights(c)
-            for prev in last_chunk:
-                invert_denominators(prev)
-            second_product(c)
-            for prev in last_chunk:
-                finish(prev)
-            last_chunk.clear()
-            last_chunk.append(c)
-
         def unit_chunks(u):
             widths = UNITS[u][3]
             return [(u, sum(widths[:i]), widths[i]) for i in range(len(widths))]
 
-        for u in range(len(UNITS)):
-            cap_scores(u)
-            if u == 0:
-                interleave(nc.vector.tensor_copy, qb[0][:], qb_raw[:])
-                gate_affine(0)
-                quantize_queries(qb, 0, Q_FIRST, NQ - Q_FIRST)
-                nc.vector.tensor_tensor(
-                    out=v_bf[:],
-                    in0=v_raw[:].rearrange("p g (j e) -> p g e j", j=PACK),
-                    in1=t_sign[:].unsqueeze(1).unsqueeze(1).to_broadcast([P, KV, E, PACK]),
-                    op=ALU.mult,
-                )
-                gate_affine(1)
-                quantize(v_codes[:], v_scales[:], v_bf[:].rearrange("p g e j -> p (g e j)"))
-                issue_scores()
-            if u == 2:
-                interleave(nc.vector.tensor_copy, qc[0][:], qc_raw[:])
-                quantize_queries(qc, 1, 0, NQ)
-                issue_scores()
-            if u > 0:
-                for c in unit_chunks(u - 1):
-                    vector_slot(c)
+        def exp_unit(u):
             for c in unit_chunks(u):
                 exp_chunk(c)
-            if u >= 2:
-                gate_tanh(u)
-        for c in unit_chunks(len(UNITS) - 1):
-            vector_slot(c)
-        for prev in last_chunk:
-            invert_denominators(prev)
-            finish(prev)
+
+        (c0,), (c1,), (c2,), (c3a, c3b), (c4,), (c5a, c5b) = [unit_chunks(u) for u in range(len(UNITS))]
+
+        cap_scores(0)
+        interleave(nc.vector.tensor_copy, qb[0][:], qb_raw[:])
+        gate_affine(0)
+        quantize_queries(qb, 0, Q_FIRST, NQ - Q_FIRST)
+        issue_scores(1)
+        nc.vector.tensor_tensor(
+            out=v_bf[:],
+            in0=v_raw[:].rearrange("p g (j e) -> p g e j", j=PACK),
+            in1=t_sign[:].unsqueeze(1).unsqueeze(1).to_broadcast([P, KV, E, PACK]),
+            op=ALU.mult,
+        )
+        exp_unit(0)
+
+        cap_scores(1)
+        group_weights(c0)
+        quantize(v_codes[:], v_scales[:], v_bf[:].rearrange("p g e j -> p (g e j)"))
+        quantize_weights(c0)
+        second_product(c0)
+        gate_affine(1)
+        exp_unit(1)
+
+        cap_scores(2)
+        interleave(nc.vector.tensor_copy, qc[0][:], qc_raw[:])
+        invert_denominators(c0)
+        quantize_queries(qc, 1, 0, NQ)
+        issue_scores(3)
+        group_weights(c1)
+        finish(c0)
+        quantize_weights(c1)
+        second_product(c1)
+        gate_affine(2)
+        exp_unit(2)
+
+        cap_scores(3)
+        group_weights(c2)
+        invert_denominators(c1)
+        quantize_weights(c2)
+        second_product(c2)
+        finish(c1)
+        invert_denominators(c2)
+        finish(c2)
+        exp_unit(3)
+        gate_tanh(3)
+
+        group_weights(c3a)
+        quantize_weights(c3a)
+        second_product(c3a)
+        group_weights(c3b)
+        invert_denominators(c3a)
+        quantize_weights(c3b)
+        second_product(c3b)
+        gate_affine(3)
+        invert_denominators(c3b)
+        finish(c3a)
+        finish(c3b)
+
+        cap_scores(4)
+        exp_unit(4)
+        gate_tanh(4)
+        group_weights(c4)
+        gate_affine(4)
+        quantize_weights(c4)
+        second_product(c4)
+        invert_denominators(c4)
+        finish(c4)
+
+        cap_scores(5)
+        exp_unit(5)
+        gate_tanh(5)
+        group_weights(c5a)
+        group_weights(c5b)
+        quantize_weights(c5a)
+        second_product(c5a)
+        quantize_weights(c5b)
+        second_product(c5b)
+        gate_affine(5)
+        invert_denominators(c5a)
+        invert_denominators(c5b)
+        finish(c5a)
+        finish(c5b)

@@ -24,11 +24,12 @@ LN_HI = 2.0 ** 64
 LN_LO = 2.0 ** -64
 TINY = 2.0 ** -126
 Q_FIRST = 256
+QUADS_ON_VECTOR = 44
 
 UNITS = [
     (0, 0, 256, [256]),
     (0, 256, 256, [256]),
-    (1, 0, 512, [512]),
+    (1, 0, 512, [256, 256]),
     (2, 0, 512, [256, 256]),
     (3, 0, 256, [256]),
     (3, 256, 256, [128, 128]),
@@ -51,6 +52,26 @@ def tile_rows_a_exp_kb_cap_gate_kernel(tc, qT, kT, t, v, kb, og, out):
                 in_=rows.rearrange("p j (c i) -> p c j i", i=PACK),
             )
 
+        def deal_pairs(engine_copy, grouped, rows, c0, c1):
+            engine_copy(
+                out=grouped.rearrange("p (b c a) j -> p c j a b", b=2, a=2)[:, c0:c1],
+                in_=rows.rearrange("p j (c a b) -> p c j a b", a=2, b=2)[:, c0:c1],
+            )
+
+        def deal_quads(grouped, rows):
+            nc.vector.tensor_copy(
+                out=grouped.rearrange("p (b m) j -> p m j b", b=PACK),
+                in_=rows.rearrange("p j (m b) -> p m j b", b=PACK),
+            )
+
+        def query_rows(dram, h, first_block, blocks):
+            if h < 2:
+                dealt = dram[h].rearrange("(g p b) e -> p g b e", p=P, b=2)
+                if blocks == 4:
+                    return dealt
+                return dealt[:, first_block // 2]
+            return dram[h].rearrange("(p b) e -> p b e", b=PACK)[:, first_block : first_block + blocks]
+
         k_pack = sb.tile([P, N + N // 4], U32, name="k_pack", align_bytes=64)
         k_swap = sb.tile([P, N + N // 4], U32, name="k_swap", align_bytes=64)
         nc.gpsimd.memset(k_pack[:, N:], 0)
@@ -61,7 +82,9 @@ def tile_rows_a_exp_kb_cap_gate_kernel(tc, qT, kT, t, v, kb, og, out):
         def load_gate(queue, u):
             h, q0, nq, chunks = UNITS[u]
             og_sb[u] = sb.tile([P, nq // NB, E], F32, name="og%d" % u)
-            queue.dma_start(out=og_sb[u][:], in_=og[h, q0 : q0 + nq, :].rearrange("(c p) e -> p c e", p=P))
+            src = query_rows(og, h, q0 // NB, nq // NB)
+            dst = og_sb[u][:].rearrange("p (g b) e -> p g b e", b=2) if src.ndim == 4 else og_sb[u][:]
+            queue.dma_start(out=dst, in_=src)
 
         t_sb = sb.tile([P, PACK], F32, name="t_sb")
         kb_sb = sb.tile([P, PACK], F32, name="kb_sb")
@@ -139,7 +162,8 @@ def tile_rows_a_exp_kb_cap_gate_kernel(tc, qT, kT, t, v, kb, og, out):
                 q_blocks[pair, q0 // NB + b] = (codes[:, b * NB : (b + 1) * NB], scales[:, b * NB : (b + 1) * NB])
 
         qa = query_tiles("qa", Q_FIRST)
-        interleave(nc.vector.tensor_copy, qa[0][:], qa_raw[:])
+        deal_pairs(nc.vector.tensor_copy, qa[0][:], qa_raw[:], 0, QUADS_ON_VECTOR)
+        deal_pairs(nc.scalar.copy, qa[0][:], qa_raw[:], QUADS_ON_VECTOR, Q_FIRST // PACK)
         gate_tanh(1)
         gate_tanh(2)
         quantize_keys(0, 1)
@@ -152,9 +176,10 @@ def tile_rows_a_exp_kb_cap_gate_kernel(tc, qT, kT, t, v, kb, og, out):
         nc.sync.dma_start(out=k_swap[HALF:, :].bitcast(I32), in_=k_pack[:HALF, :].bitcast(I32))
         qc_raw = sb.tile([P, PACK, NQ], F32, name="qc_raw")
         nc.sync.dma_start(out=qc_raw[:], in_=q_rows[1])
+        load_gate(nc.sync, 4)
         nc.sync.dma_start(out=k_swap[:HALF, :].bitcast(I32), in_=k_pack[HALF:, :].bitcast(I32))
-        for u in range(3, len(UNITS)):
-            load_gate(nc.sync, u)
+        load_gate(nc.sync, 3)
+        load_gate(nc.sync, 5)
 
         qb = query_tiles("qb", NQ - Q_FIRST)
         qc = query_tiles("qc", NQ)
@@ -163,7 +188,7 @@ def tile_rows_a_exp_kb_cap_gate_kernel(tc, qT, kT, t, v, kb, og, out):
         v_scales = sb.tile([P, KV * E], U8, name="v_scales", align_bytes=64)
 
         def bank_groups(u):
-            if u == 0:
+            if UNITS[u][0] == 0:
                 return [(0,), (1,), (2, 3)]
             per_bank = 4 * NB // UNITS[u][2]
             return [tuple(range(r, r + per_bank)) for r in range(0, PACK, per_bank)]
@@ -201,24 +226,25 @@ def tile_rows_a_exp_kb_cap_gate_kernel(tc, qT, kT, t, v, kb, og, out):
 
         capped = {}
 
-        def cap_scores(u):
+        def cap_scores(u, gate_unit=None):
             h, q0, nq, chunks = UNITS[u]
             capped[u] = sb.tile([P, PACK, nq], F32, name="cap%d" % u)
             for places in bank_groups(u):
-                issue_scores(u + 1)
+                issue_scores(u)
+                if gate_unit is not None and PACK - 1 in places:
+                    gate_tanh(gate_unit)
                 for r in places:
                     nc.scalar.activation(
                         out=capped[u][:, r, :], in_=banks[u, r], func=ACT.Tanh, bias=kb_cap[:, r : r + 1], scale=1.0 / CAP
                     )
                 free_banks[h % 2] = free_banks[h % 2] + 1
-            issue_scores(u + 1)
 
         weights = {}
 
         def exp_chunk(c):
             u, c0, n = c
             weights[c] = sb.tile([P, PACK, n], BF16, name="w%d_%d" % (u, c0))
-            for r in range(PACK):
+            for r in (1, 0, 3, 2):
                 nc.scalar.activation(
                     out=weights[c][:, r, :], in_=capped[u][:, r, c0 : c0 + n], func=ACT.Exp, bias=ln_t[:, r : r + 1], scale=CAP
                 )
@@ -258,7 +284,7 @@ def tile_rows_a_exp_kb_cap_gate_kernel(tc, qT, kT, t, v, kb, og, out):
             inv_den[c] = sb.tile([P, n // NB], F32, name="inv%d_%d" % (u, c0))
             nc.vector.reciprocal(out=inv_den[c][:], in_=y_banks[c][:, : n // NB, E - 1])
 
-        def finish(c):
+        def finish(c, queue=nc.sync):
             u, c0, n = c
             h, q0, nq, chunks = UNITS[u]
             res = sb.tile([P, n // NB, E], F32, name="res%d_%d" % (u, c0))
@@ -271,7 +297,7 @@ def tile_rows_a_exp_kb_cap_gate_kernel(tc, qT, kT, t, v, kb, og, out):
                     op0=ALU.mult,
                     op1=ALU.mult,
                 )
-            nc.sync.dma_start(out=out[h, q0 + c0 : q0 + c0 + n, :].rearrange("(c p) e -> p c e", p=P), in_=res[:])
+            queue.dma_start(out=query_rows(out, h, (q0 + c0) // NB, n // NB), in_=res[:])
 
         def unit_chunks(u):
             widths = UNITS[u][3]
@@ -281,10 +307,10 @@ def tile_rows_a_exp_kb_cap_gate_kernel(tc, qT, kT, t, v, kb, og, out):
             for c in unit_chunks(u):
                 exp_chunk(c)
 
-        (c0,), (c1,), (c2,), (c3a, c3b), (c4,), (c5a, c5b) = [unit_chunks(u) for u in range(len(UNITS))]
+        (c0,), (c1,), (c2a, c2b), (c3a, c3b), (c4,), (c5a, c5b) = [unit_chunks(u) for u in range(len(UNITS))]
 
         cap_scores(0)
-        interleave(nc.vector.tensor_copy, qb[0][:], qb_raw[:])
+        deal_pairs(nc.vector.tensor_copy, qb[0][:], qb_raw[:], 0, Q_FIRST // PACK)
         gate_affine(0)
         quantize_queries(qb, 0, Q_FIRST, NQ - Q_FIRST)
         issue_scores(1)
@@ -297,6 +323,7 @@ def tile_rows_a_exp_kb_cap_gate_kernel(tc, qT, kT, t, v, kb, og, out):
         exp_unit(0)
 
         cap_scores(1)
+        issue_scores(2)
         group_weights(c0)
         quantize(v_codes[:], v_scales[:], v_bf[:].rearrange("p g e j -> p (g e j)"))
         quantize_weights(c0)
@@ -304,8 +331,8 @@ def tile_rows_a_exp_kb_cap_gate_kernel(tc, qT, kT, t, v, kb, og, out):
         gate_affine(1)
         exp_unit(1)
 
-        cap_scores(2)
-        interleave(nc.vector.tensor_copy, qc[0][:], qc_raw[:])
+        cap_scores(2, 4)
+        deal_quads(qc[0][:], qc_raw[:])
         invert_denominators(c0)
         quantize_queries(qc, 1, 0, NQ)
         issue_scores(3)
@@ -314,52 +341,57 @@ def tile_rows_a_exp_kb_cap_gate_kernel(tc, qT, kT, t, v, kb, og, out):
         quantize_weights(c1)
         second_product(c1)
         gate_affine(2)
+        gate_affine(4)
         exp_unit(2)
-
-        cap_scores(3)
-        group_weights(c2)
+        group_weights(c2a)
         invert_denominators(c1)
-        quantize_weights(c2)
-        second_product(c2)
+        quantize_weights(c2a)
+        second_product(c2a)
         finish(c1)
-        invert_denominators(c2)
-        finish(c2)
-        exp_unit(3)
-        gate_tanh(3)
+        group_weights(c2b)
+        invert_denominators(c2a)
+        quantize_weights(c2b)
 
+        cap_scores(3, 3)
+        second_product(c2b)
+        issue_scores(4)
+        finish(c2a)
+        invert_denominators(c2b)
+        finish(c2b)
+        issue_scores(5)
+        exp_unit(3)
         group_weights(c3a)
+        gate_affine(3)
         quantize_weights(c3a)
         second_product(c3a)
         group_weights(c3b)
         invert_denominators(c3a)
         quantize_weights(c3b)
         second_product(c3b)
-        gate_affine(3)
-        invert_denominators(c3b)
-        finish(c3a)
-        finish(c3b)
 
         cap_scores(4)
+        issue_scores(5)
+        finish(c3a)
         exp_unit(4)
-        gate_tanh(4)
         group_weights(c4)
-        gate_affine(4)
+        invert_denominators(c3b)
         quantize_weights(c4)
         second_product(c4)
-        invert_denominators(c4)
-        finish(c4)
+        finish(c3b)
 
         cap_scores(5)
         exp_unit(5)
         gate_tanh(5)
         group_weights(c5a)
-        group_weights(c5b)
+        invert_denominators(c4)
         quantize_weights(c5a)
         second_product(c5a)
+        group_weights(c5b)
+        finish(c4)
         quantize_weights(c5b)
         second_product(c5b)
         gate_affine(5)
         invert_denominators(c5a)
-        invert_denominators(c5b)
         finish(c5a)
-        finish(c5b)
+        invert_denominators(c5b)
+        finish(c5b, nc.scalar)

from contextlib import ExitStack

import concourse.mybir as mybir

H, KV, D, NQ, N, E = 4, 2, 256, 512, 512, 128
CAP = 2.0
FLOPS = 2 * H * NQ * N * (D + E)

F32 = mybir.dt.float32
BF16 = mybir.dt.bfloat16
U32 = mybir.dt.uint32
I32 = mybir.dt.int32
U8 = mybir.dt.uint8
FP8X4 = mybir.dt.float8_e4m3fn_x4
ACT = mybir.ActivationFunctionType
ALU = mybir.AluOpType

P = 128
HALF = 64
PACK = 4
NB = 128
SCORE_BANKS = 3
LN_HI = 2.0 ** 64
LN_LO = 2.0 ** -64
TINY = 2.0 ** -126
Q_FIRST = 256
QUADS_ON_VECTOR = 44

UNITS = [
    (0, 0, 256, [256]),
    (0, 256, 256, [256]),
    (1, 0, 512, [256, 256]),
    (2, 0, 512, [256, 256]),
    (3, 0, 256, [256]),
    (3, 256, 256, [128, 128]),
]


def tile_rows_a_exp_kb_cap_gate_kernel(tc, qT, kT, t, v, kb, og, out):
    nc = tc.nc
    with ExitStack() as ctx:
        sb = ctx.enter_context(tc.tile_pool(name="sb", bufs=1))
        ps = ctx.enter_context(tc.psum_pool(name="ps", bufs=1))
        ctx.enter_context(tc.manual_schedule())

        def quantize(codes, scales, grouped):
            nc.vector.quantize_mx(out=codes.bitcast(FP8X4), scales=scales, in_=grouped)

        def interleave(engine_copy, grouped, rows):
            engine_copy(
                out=grouped.rearrange("p (c i) j -> p c j i", i=PACK),
                in_=rows.rearrange("p j (c i) -> p c j i", i=PACK),
            )

        def deal_pairs(engine_copy, grouped, rows, c0, c1):
            engine_copy(
                out=grouped.rearrange("p (b c a) j -> p c j a b", b=2, a=2)[:, c0:c1],
                in_=rows.rearrange("p j (c a b) -> p c j a b", a=2, b=2)[:, c0:c1],
            )

        def deal_quads(grouped, rows):
            nc.vector.tensor_copy(
                out=grouped.rearrange("p (b m) j -> p m j b", b=PACK),
                in_=rows.rearrange("p j (m b) -> p m j b", b=PACK),
            )

        def query_rows(dram, h, first_block, blocks):
            if h < 2:
                dealt = dram[h].rearrange("(g p b) e -> p g b e", p=P, b=2)
                if blocks == 4:
                    return dealt
                return dealt[:, first_block // 2]
            return dram[h].rearrange("(p b) e -> p b e", b=PACK)[:, first_block : first_block + blocks]

        k_pack = sb.tile([P, N + N // 4], U32, name="k_pack", align_bytes=64)
        k_swap = sb.tile([P, N + N // 4], U32, name="k_swap", align_bytes=64)
        nc.gpsimd.memset(k_pack[:, N:], 0)

        q_rows = qT.rearrange("(g h) (p j) n -> g (h p) j n", h=2, j=PACK)
        og_sb = {}

        def load_gate(queue, u):
            h, q0, nq, chunks = UNITS[u]
            og_sb[u] = sb.tile([P, nq // NB, E], F32, name="og%d" % u)
            src = query_rows(og, h, q0 // NB, nq // NB)
            dst = og_sb[u][:].rearrange("p (g b) e -> p g b e", b=2) if src.ndim == 4 else og_sb[u][:]
            queue.dma_start(out=dst, in_=src)

        t_sb = sb.tile([P, PACK], F32, name="t_sb")
        kb_sb = sb.tile([P, PACK], F32, name="kb_sb")
        nc.sync.dma_start(out=t_sb[:], in_=t.rearrange("(p j) o -> p (j o)", j=PACK))
        nc.scalar.dma_start(out=kb_sb[:], in_=kb.rearrange("(p j) o -> p (j o)", j=PACK))
        load_gate(nc.scalar, 0)

        k_raw = sb.tile([P, PACK, N], F32, name="k_raw")
        nc.sync.dma_start(out=k_raw[:], in_=kT.rearrange("g (p j) n -> (g p) j n", j=PACK))
        qa_raw = sb.tile([P, PACK, Q_FIRST], F32, name="qa_raw")
        nc.sync.dma_start(out=qa_raw[:], in_=q_rows[0][:, :, :Q_FIRST])
        load_gate(nc.sync, 1)
        load_gate(nc.sync, 2)
        qb_raw = sb.tile([P, PACK, NQ - Q_FIRST], F32, name="qb_raw")
        nc.sync.dma_start(out=qb_raw[:], in_=q_rows[0][:, :, Q_FIRST:])

        t_abs = sb.tile([P, PACK], F32, name="t_abs")
        nc.vector.scalar_tensor_tensor(out=t_abs[:], in0=t_sb[:], scalar=-1.0, in1=t_sb[:], op0=ALU.mult, op1=ALU.max)
        t_pos = sb.tile([P, PACK], F32, name="t_pos")
        nc.vector.tensor_scalar(out=t_pos[:], in0=t_sb[:], scalar1=0.0, scalar2=2.0, op0=ALU.is_ge, op1=ALU.mult)
        t_rng = sb.tile([P, 3, PACK], F32, name="t_rng")
        nc.vector.tensor_scalar(out=t_rng[:, 0, :], in0=t_abs[:], scalar1=LN_LO, scalar2=LN_HI, op0=ALU.max, op1=ALU.min)
        nc.vector.tensor_scalar(out=t_rng[:, 1, :], in0=t_abs[:], scalar1=LN_HI, scalar2=LN_LO, op0=ALU.max, op1=ALU.mult)
        nc.vector.tensor_scalar(out=t_rng[:, 2, :], in0=t_abs[:], scalar1=TINY, scalar2=LN_LO, op0=ALU.max, op1=ALU.min)
        t_sign = sb.tile([P, PACK], F32, name="t_sign")
        nc.vector.tensor_scalar(out=t_sign[:], in0=t_pos[:], scalar1=-1.0, scalar2=None, op0=ALU.add)
        kb_cap = sb.tile([P, PACK], F32, name="kb_cap")
        nc.vector.tensor_scalar(out=kb_cap[:], in0=kb_sb[:], scalar1=1.0 / CAP, scalar2=None, op0=ALU.mult)
        ln_rng = sb.tile([P, 3, PACK], F32, name="ln_rng")
        nc.scalar.activation(out=ln_rng[:, 0:2, :], in_=t_rng[:, 0:2, :], func=ACT.Ln)
        nc.scalar.activation(out=ln_rng[:, 2, :], in_=t_rng[:, 2, :], func=ACT.Ln, scale=LN_HI)
        ln_t = sb.tile([P, PACK], F32, name="ln_t")

        half_tanh = {}
        gate = {}

        def gate_tanh(u):
            half_tanh[u] = sb.tile([P, UNITS[u][2] // NB, E], F32, name="gt%d" % u)
            nc.scalar.activation(out=half_tanh[u][:], in_=og_sb[u][:], func=ACT.Tanh, scale=0.5)

        def gate_affine(u):
            gate[u] = sb.tile([P, UNITS[u][2] // NB, E], F32, name="gate%d" % u)
            nc.vector.tensor_scalar(out=gate[u][:], in0=half_tanh[u][:], scalar1=0.5, scalar2=0.5, op0=ALU.mult, op1=ALU.add)

        gate_tanh(0)

        k_bf = sb.tile([P, PACK, NB, PACK], BF16, name="k_bf", align_bytes=64)
        nc.vector.tensor_copy(
            out=k_bf[:].rearrange("p r s j -> p s j r"),
            in_=k_raw[:].rearrange("p j (s r) -> p s j r", r=PACK),
        )
        nc.vector.tensor_reduce(out=ln_t[:], in_=ln_rng[:].rearrange("p a j -> p j a"), axis=mybir.AxisListType.X, op=ALU.add)

        def k_codes(pack, r0, r1):
            return pack[:, r0 * NB : r1 * NB]

        def k_scales(pack, r0, r1):
            return pack[:, N + r0 * NB // 4 : N + r1 * NB // 4].bitcast(U8)

        def quantize_keys(r0, r1):
            quantize(k_codes(k_pack, r0, r1), k_scales(k_pack, r0, r1), k_bf[:, r0:r1].rearrange("p r s j -> p (r s j)"))

        q_blocks = {}

        def query_tiles(name, n):
            grouped = sb.tile([P, n, PACK], BF16, name=name + "_bf", align_bytes=64)
            codes = sb.tile([P, n], U32, name=name + "_codes", align_bytes=64)
            scales = sb.tile([P, n], U8, name=name + "_scales", align_bytes=64)
            return grouped, codes, scales

        def quantize_queries(tiles, pair, q0, n):
            grouped, codes, scales = tiles
            quantize(codes[:], scales[:], grouped[:].rearrange("p n j -> p (n j)"))
            for b in range(n // NB):
                q_blocks[pair, q0 // NB + b] = (codes[:, b * NB : (b + 1) * NB], scales[:, b * NB : (b + 1) * NB])

        qa = query_tiles("qa", Q_FIRST)
        deal_pairs(nc.vector.tensor_copy, qa[0][:], qa_raw[:], 0, QUADS_ON_VECTOR)
        deal_pairs(nc.scalar.copy, qa[0][:], qa_raw[:], QUADS_ON_VECTOR, Q_FIRST // PACK)
        gate_tanh(1)
        gate_tanh(2)
        quantize_keys(0, 1)
        quantize_queries(qa, 0, 0, Q_FIRST)
        quantize_keys(1, 2)
        quantize_keys(2, 4)

        v_raw = sb.tile([P, KV, PACK * E], F32, name="v_raw")
        nc.sync.dma_start(out=v_raw[:], in_=v.rearrange("g (p j) e -> p g (j e)", j=PACK))
        nc.sync.dma_start(out=k_swap[HALF:, :].bitcast(I32), in_=k_pack[:HALF, :].bitcast(I32))
        qc_raw = sb.tile([P, PACK, NQ], F32, name="qc_raw")
        nc.sync.dma_start(out=qc_raw[:], in_=q_rows[1])
        load_gate(nc.sync, 4)
        nc.sync.dma_start(out=k_swap[:HALF, :].bitcast(I32), in_=k_pack[HALF:, :].bitcast(I32))
        load_gate(nc.sync, 3)
        load_gate(nc.sync, 5)

        qb = query_tiles("qb", NQ - Q_FIRST)
        qc = query_tiles("qc", NQ)
        v_bf = sb.tile([P, KV, E, PACK], BF16, name="v_bf", align_bytes=64)
        v_codes = sb.tile([P, KV * E], U32, name="v_codes", align_bytes=64)
        v_scales = sb.tile([P, KV * E], U8, name="v_scales", align_bytes=64)

        def bank_groups(u):
            if UNITS[u][0] == 0:
                return [(0,), (1,), (2, 3)]
            per_bank = 4 * NB // UNITS[u][2]
            return [tuple(range(r, r + per_bank)) for r in range(0, PACK, per_bank)]

        banks = {}
        free_banks = [SCORE_BANKS, SCORE_BANKS]
        pending = [(u, places) for u in range(len(UNITS)) for places in bank_groups(u)]

        def issue_scores(last_unit):
            while pending and pending[0][0] <= last_unit:
                u, places = pending[0]
                h, q0, nq, chunks = UNITS[u]
                side = h % 2
                blocks = [(h // 2, b) for b in range(q0 // NB, (q0 + nq) // NB)]
                if free_banks[side] == 0 or any(b not in q_blocks for b in blocks):
                    return
                pending.remove((u, places))
                free_banks[side] = free_banks[side] - 1
                rows = slice(side * HALF, (side + 1) * HALF)
                pack = k_pack if side == h // 2 else k_swap
                bank = ps.tile([P, 4 * NB], F32, name="scores%d" % side, tag="scores%d" % side, bufs=SCORE_BANKS)
                for slot, r in enumerate(places):
                    banks[u, r] = bank[:, slot * nq : (slot + 1) * nq]
                    for i, b in enumerate(blocks):
                        codes, scales = q_blocks[b]
                        nc.tensor.matmul_mx(
                            out=banks[u, r][:, i * NB : (i + 1) * NB],
                            lhsT=k_codes(pack, r, r + 1)[rows, :].bitcast(FP8X4),
                            lhsT_scale=k_scales(pack, r, r + 1)[rows, :],
                            rhs=codes[rows, :].bitcast(FP8X4),
                            rhs_scale=scales[rows, :],
                            start=True,
                            stop=True,
                        )

        capped = {}

        def cap_scores(u, gate_unit=None):
            h, q0, nq, chunks = UNITS[u]
            capped[u] = sb.tile([P, PACK, nq], F32, name="cap%d" % u)
            for places in bank_groups(u):
                issue_scores(u)
                if gate_unit is not None and PACK - 1 in places:
                    gate_tanh(gate_unit)
                for r in places:
                    nc.scalar.activation(
                        out=capped[u][:, r, :], in_=banks[u, r], func=ACT.Tanh, bias=kb_cap[:, r : r + 1], scale=1.0 / CAP
                    )
                free_banks[h % 2] = free_banks[h % 2] + 1

        weights = {}

        def exp_chunk(c):
            u, c0, n = c
            weights[c] = sb.tile([P, PACK, n], BF16, name="w%d_%d" % (u, c0))
            for r in (1, 0, 3, 2):
                nc.scalar.activation(
                    out=weights[c][:, r, :], in_=capped[u][:, r, c0 : c0 + n], func=ACT.Exp, bias=ln_t[:, r : r + 1], scale=CAP
                )

        w_tiles = {}
        y_banks = {}
        inv_den = {}

        def group_weights(c):
            u, c0, n = c
            w_tiles[c] = query_tiles("wq%d_%d" % (u, c0), n)
            interleave(nc.vector.tensor_copy, w_tiles[c][0][:], weights[c][:])

        def quantize_weights(c):
            grouped, codes, scales = w_tiles[c]
            quantize(codes[:], scales[:], grouped[:].rearrange("p n j -> p (n j)"))

        def second_product(c):
            u, c0, n = c
            g = UNITS[u][0] // 2
            grouped, codes, scales = w_tiles[c]
            y = ps.tile([P, 4, E], F32, name="y", tag="y", bufs=2)
            y_banks[c] = y
            for b in range(n // NB):
                nc.tensor.matmul_mx(
                    out=y[:, b, :],
                    lhsT=codes[:, b * NB : (b + 1) * NB].bitcast(FP8X4),
                    lhsT_scale=scales[:, b * NB : (b + 1) * NB],
                    rhs=v_codes[:, g * E : (g + 1) * E].bitcast(FP8X4),
                    rhs_scale=v_scales[:, g * E : (g + 1) * E],
                    start=True,
                    stop=True,
                )

        def invert_denominators(c):
            u, c0, n = c
            inv_den[c] = sb.tile([P, n // NB], F32, name="inv%d_%d" % (u, c0))
            nc.vector.reciprocal(out=inv_den[c][:], in_=y_banks[c][:, : n // NB, E - 1])

        def finish(c, queue=nc.sync):
            u, c0, n = c
            h, q0, nq, chunks = UNITS[u]
            res = sb.tile([P, n // NB, E], F32, name="res%d_%d" % (u, c0))
            for b in range(n // NB):
                nc.vector.scalar_tensor_tensor(
                    out=res[:, b, :],
                    in0=y_banks[c][:, b, :],
                    scalar=inv_den[c][:, b : b + 1],
                    in1=gate[u][:, c0 // NB + b, :],
                    op0=ALU.mult,
                    op1=ALU.mult,
                )
            queue.dma_start(out=query_rows(out, h, (q0 + c0) // NB, n // NB), in_=res[:])

        def unit_chunks(u):
            widths = UNITS[u][3]
            return [(u, sum(widths[:i]), widths[i]) for i in range(len(widths))]

        def exp_unit(u):
            for c in unit_chunks(u):
                exp_chunk(c)

        (c0,), (c1,), (c2a, c2b), (c3a, c3b), (c4,), (c5a, c5b) = [unit_chunks(u) for u in range(len(UNITS))]

        cap_scores(0)
        deal_pairs(nc.vector.tensor_copy, qb[0][:], qb_raw[:], 0, Q_FIRST // PACK)
        gate_affine(0)
        quantize_queries(qb, 0, Q_FIRST, NQ - Q_FIRST)
        issue_scores(1)
        nc.vector.tensor_tensor(
            out=v_bf[:],
            in0=v_raw[:].rearrange("p g (j e) -> p g e j", j=PACK),
            in1=t_sign[:].unsqueeze(1).unsqueeze(1).to_broadcast([P, KV, E, PACK]),
            op=ALU.mult,
        )
        exp_unit(0)

        cap_scores(1)
        issue_scores(2)
        group_weights(c0)
        quantize(v_codes[:], v_scales[:], v_bf[:].rearrange("p g e j -> p (g e j)"))
        quantize_weights(c0)
        second_product(c0)
        gate_affine(1)
        exp_unit(1)

        cap_scores(2, 4)
        deal_quads(qc[0][:], qc_raw[:])
        invert_denominators(c0)
        quantize_queries(qc, 1, 0, NQ)
        issue_scores(3)
        group_weights(c1)
        finish(c0)
        quantize_weights(c1)
        second_product(c1)
        gate_affine(2)
        gate_affine(4)
        exp_unit(2)
        group_weights(c2a)
        invert_denominators(c1)
        quantize_weights(c2a)
        second_product(c2a)
        finish(c1)
        group_weights(c2b)
        invert_denominators(c2a)
        quantize_weights(c2b)

        cap_scores(3, 3)
        second_product(c2b)
        issue_scores(4)
        finish(c2a)
        invert_denominators(c2b)
        finish(c2b)
        issue_scores(5)
        exp_unit(3)
        group_weights(c3a)
        gate_affine(3)
        quantize_weights(c3a)
        second_product(c3a)
        group_weights(c3b)
        invert_denominators(c3a)
        quantize_weights(c3b)
        second_product(c3b)

        cap_scores(4)
        issue_scores(5)
        finish(c3a)
        exp_unit(4)
        group_weights(c4)
        invert_denominators(c3b)
        quantize_weights(c4)
        second_product(c4)
        finish(c3b)

        cap_scores(5)
        exp_unit(5)
        gate_tanh(5)
        group_weights(c5a)
        invert_denominators(c4)
        quantize_weights(c5a)
        second_product(c5a)
        group_weights(c5b)
        finish(c4)
        quantize_weights(c5b)
        second_product(c5b)
        gate_affine(5)
        invert_denominators(c5a)
        finish(c5a)
        invert_denominators(c5b)
        finish(c5b, nc.scalar)
